import numpy as np, ml_dtypes
CORES = [2,10,50,58,66,74,122]
N = 7
QP = 32
def setup_inputs(rng):
    return {"q": rng.standard_normal((N, 128, QP), dtype=np.float32).astype(ml_dtypes.bfloat16), "k": rng.standard_normal((N, 128, 128), dtype=np.float32).astype(ml_dtypes.bfloat16), "v": rng.standard_normal((N, 128, 128), dtype=np.float32).astype(ml_dtypes.bfloat16)}
def setup_inputs_big(rng):
    d = setup_inputs(rng)
    for k in ("q", "k", "v"): d[k] = (d[k].astype(np.float32) * 1024.0).astype(d[k].dtype)
    return d
def setup_inputs_small(rng):
    d = setup_inputs(rng)
    for k in ("q", "k", "v"): d[k] = (d[k].astype(np.float32) * (1 / 1024.0)).astype(d[k].dtype)
    return d
def setup_inputs_apart(rng):
    d = setup_inputs(rng)
    f = (10.0 ** rng.permutation(np.linspace(-1.5, 1.5, N))).astype(np.float32).reshape(N, 1, 1)
    for k in ("q", "k", "v"): d[k] = (d[k].astype(np.float32) * f).astype(d[k].dtype)
    return d
def reference(q, k, v):
    Q, K, V = q.astype(np.float64), k.astype(np.float64), v.astype(np.float64)
    y = np.zeros((N, 128, QP))
    for r in range(N):
        S = [K[j].T @ Q[r] for j in range(N)]
        m = np.max([s.max(axis=0) for s in S], axis=0)
        y[r] = sum(V[j].T @ np.maximum(S[j] - 0.5 * m, 0.0) for j in range(N))
    return {"y": y.astype(ml_dtypes.bfloat16)}

@@ -1,0 +1,132 @@
+from concourse.bass import DstId, RemoteDMATransfer
+from concourse.mybir import dt, AluOpType
+
+N = 7
+QP = 32
+KP = 128
+SLOT = 2 * KP
+
+SCRATCH = {
+    "land": ("sbuf", [128, N * SLOT], "bfloat16"),
+    "qs": ("sbuf", [128, QP], "bfloat16"),
+    "stair": ("sbuf", [128, QP + 1], "bfloat16"),
+    "diag": ("sbuf", [128, QP], "bfloat16"),
+    "ones": ("sbuf", [128, KP], "bfloat16"),
+    "zeros": ("sbuf", [128, QP], "float32"),
+    "run": ("sbuf", [128, N * KP], "float32"),
+    "tree": ("sbuf", [128, KP], "float32"),
+    "mcol": ("sbuf", [128, 8], "bfloat16"),
+    "mrow": ("sbuf", [128, QP], "bfloat16"),
+    "p": ("sbuf", [128, N * QP], "bfloat16"),
+    "ysb": ("sbuf", [128, QP], "bfloat16"),
+    "pm": ("psum", [128, 512], "float32"),
+}
+for _j in range(N):
+    SCRATCH["ps%d" % _j] = ("psum", [128, 512], "float32")
+
+SEMAPHORES = (["ldk", "ldv", "ldq", "sent", "stored", "fill0", "fill", "idn", "row", "mr", "yd", "yc"]
+              + ["arr%d" % j for j in range(N)] + ["st%d" % j for j in range(N)] + ["mx%d" % j for j in range(N)]
+              + ["tr%d" % j for j in range(7)] + ["bi%d" % j for j in range(N)] + ["rl%d" % j for j in range(N)])
+
+
+def rank_program(g, core, T, topo):
+    rank = T.rank_of(core)
+    if rank is None:
+        return
+    cores = T.cores
+    n = len(cores)
+    sem = T.sem
+    te, ve = g.tensor, g.vector
+
+    def kslot(j):
+        return T.land[:, j * SLOT:j * SLOT + KP]
+
+    def vslot(j):
+        return T.land[:, j * SLOT + KP:(j + 1) * SLOT]
+
+    own = T.land[:, rank * SLOT:(rank + 1) * SLOT]
+
+    g.sync.dma_start(kslot(rank), T.k[:]).then_inc(sem.ldk, 16)
+    g.scalar.dma_start(vslot(rank), T.v[:]).then_inc(sem.ldv, 16)
+    g.sync.dma_start(T.qs[:], T.q[:]).then_inc(sem.ldq, 16)
+
+    dests = [(rank + i) % n for i in range(1, n)]
+    mask = topo.mask(core, cores[dests[0]])
+    for d in dests:
+        mask &= topo.mask(core, cores[d])
+    eng = bin(mask).count("1")
+    ids = []
+    for d in dests:
+        rid, pid, _se = topo.addr(cores[d])
+        ids.append(DstId(rid=rid, pnc=pid))
+    g.wait_ge(sem.ldk, 16)
+    g.wait_ge(sem.ldv, 16)
+    g.remote_dma_fused(
+        [RemoteDMATransfer(dst_ids=ids, dma_engine_mask=mask, remote_sem=sem["arr%d" % rank],
+                           srcs=[own], dsts=[own for _d in dests])],
+        local_sem=sem.sent)
+
+    ve.memset(T.stair[0:QP, :], 0.0).then_inc(sem.fill0, 1)
+    ve.memset(T.ones[0:1, :], 1.0).then_inc(sem.fill, 1)
+    ve.memset(T.zeros[:], 0.0).then_inc(sem.fill, 1)
+    ve.wait_ge(sem.fill0, 1)
+    for c in range(QP):
+        ve.memset(T.stair[0:c + 1, c + 1:c + 2], -0.5).then_inc(sem.fill, 1)
+    ve.wait_ge(sem.fill, QP + 2)
+    ve.tensor_tensor(T.diag[0:QP, :], T.stair[0:QP, 1:QP + 1], T.stair[0:QP, 0:QP], AluOpType.subtract).then_inc(sem.idn, 1)
+
+    order = [rank] + [(rank - i) % n for i in range(1, n)]
+    st_ap = T.pm[0:QP, 0:KP]
+    for i, j in enumerate(order):
+        if j == rank:
+            te.wait_ge(sem.ldk, 16)
+            te.wait_ge(sem.ldq, 16)
+        else:
+            te.wait_ge(sem["arr%d" % j], eng)
+        if i > 0:
+            te.wait_ge(sem["mx%d" % (i - 1)], 1)
+        te.matmul(st_ap, T.qs[:], kslot(j), True, True).then_inc(sem["st%d" % i], 1)
+        te.matmul(T["ps%d" % j][:, 0:QP], kslot(j), T.qs[:], True, False)
+        ve.wait_ge(sem["st%d" % i], 1)
+        blk = T.run[0:QP, i * KP:(i + 1) * KP]
+        if i == 0:
+            ve.tensor_copy(blk, st_ap).then_inc(sem["mx%d" % i], 1)
+        else:
+            ve.wait_ge(sem["mx%d" % (i - 1)], 1)
+            ve.tensor_tensor(blk, st_ap, T.run[0:QP, (i - 1) * KP:i * KP], AluOpType.max).then_inc(sem["mx%d" % i], 1)
+
+    ve.wait_ge(sem["mx%d" % (n - 1)], 1)
+    src, lo, w, off, step = T.run, (n - 1) * KP, KP // 2, 0, 0
+    while w >= 1:
+        out = T.tree[0:QP, off:off + w] if w > 1 else T.mcol[0:QP, 0:1]
+        ve.tensor_tensor(out, src[0:QP, lo:lo + w], src[0:QP, lo + w:lo + 2 * w], AluOpType.max).then_inc(sem["tr%d" % step], 1)
+        ve.wait_ge(sem["tr%d" % step], 1)
+        src, lo, off, w, step = T.tree, off, off + w, w // 2, step + 1
+
+    row_ap = T.pm[0:1, KP:KP + QP]
+    te.wait_ge(sem["tr%d" % (step - 1)], 1)
+    te.wait_ge(sem.idn, 1)
+    te.wait_ge(sem.fill, QP + 2)
+    te.matmul(row_ap, T.mcol[0:QP, 0:1], T.diag[0:QP, :], True, True).then_inc(sem.row, 1)
+    ve.wait_ge(sem.row, 1)
+    ve.tensor_copy(T.mrow[0:1, :], row_ap).then_inc(sem.mr, 1)
+    te.wait_ge(sem.mr, 1)
+    for j in order:
+        te.matmul(T["ps%d" % j][:, 0:QP], T.ones[0:1, :], T.mrow[0:1, :], False, True).then_inc(sem["bi%d" % j], 1)
+    for j in order:
+        ve.wait_ge(sem["bi%d" % j], 1)
+        ve.tensor_tensor(T.p[:, j * QP:(j + 1) * QP], T["ps%d" % j][:, 0:QP], T.zeros[:], AluOpType.max).then_inc(sem["rl%d" % j], 1)
+
+    y_ap = T.pm[:, 2 * KP:2 * KP + QP]
+    te.wait_ge(sem.ldv, 16)
+    last = None
+    for i, j in enumerate(order):
+        te.wait_ge(sem["rl%d" % j], 1)
+        last = te.matmul(y_ap, vslot(j), T.p[:, j * QP:(j + 1) * QP], i == 0, i == n - 1)
+    last.then_inc(sem.yd, 1)
+    ve.wait_ge(sem.yd, 1)
+    ve.tensor_copy(T.ysb[:], y_ap).then_inc(sem.yc, 1)
+    g.sync.wait_ge(sem.yc, 1)
+    g.sync.dma_start(T.y[:], T.ysb[:]).then_inc(sem.stored, 16)
+    g.sync.wait_ge(sem.stored, 16)
+    g.wait_ge(sem.sent, eng)

@@ -4,29 +4,36 @@ from concourse.mybir import dt, AluOpType
 N = 7
 QP = 32
 KP = 128
-SLOT = 2 * KP
+NB = (N + 1) // 2
+NT = 3
 
 SCRATCH = {
-    "land": ("sbuf", [128, N * SLOT], "bfloat16"),
+    "kall": ("sbuf", [128, N * KP], "bfloat16"),
+    "vall": ("sbuf", [128, N * KP], "bfloat16"),
     "qs": ("sbuf", [128, QP], "bfloat16"),
     "stair": ("sbuf", [128, QP + 1], "bfloat16"),
-    "diag": ("sbuf", [128, QP], "bfloat16"),
+    "diag": ("sbuf", [128, 2 * QP], "bfloat16"),
     "ones": ("sbuf", [128, KP], "bfloat16"),
-    "zeros": ("sbuf", [128, QP], "float32"),
-    "run": ("sbuf", [128, N * KP], "float32"),
+    "zrow": ("sbuf", [128, 2 * QP], "bfloat16"),
+    "zeros": ("sbuf", [128, 2 * QP], "float32"),
+    "run": ("sbuf", [128, 2 * N * KP], "float32"),
     "tree": ("sbuf", [128, KP], "float32"),
     "mcol": ("sbuf", [128, 8], "bfloat16"),
-    "mrow": ("sbuf", [128, QP], "bfloat16"),
-    "p": ("sbuf", [128, N * QP], "bfloat16"),
+    "mrow": ("sbuf", [128, 2 * QP], "bfloat16"),
+    "p": ("sbuf", [128, 2 * NB * QP], "bfloat16"),
     "ysb": ("sbuf", [128, QP], "bfloat16"),
     "pm": ("psum", [128, 512], "float32"),
 }
-for _j in range(N):
-    SCRATCH["ps%d" % _j] = ("psum", [128, 512], "float32")
+for _j in range(NB):
+    SCRATCH["sb%d" % _j] = ("psum", [128, 512], "float32")
+for _j in range(NT):
+    SCRATCH["tb%d" % _j] = ("psum", [128, 512], "float32")
 
-SEMAPHORES = (["ldk", "ldv", "ldq", "sent", "stored", "fill0", "fill", "idn", "row", "mr", "yd", "yc"]
-              + ["arr%d" % j for j in range(N)] + ["st%d" % j for j in range(N)] + ["mx%d" % j for j in range(N)]
-              + ["tr%d" % j for j in range(7)] + ["bi%d" % j for j in range(N)] + ["rl%d" % j for j in range(N)])
+SEMAPHORES = (["ldk", "ldv", "ldq", "sent", "stored", "fillc", "fill0", "fill", "idn", "row", "mr", "yd", "yc"]
+              + ["ka%d" % j for j in range(N)] + ["va%d" % j for j in range(N)]
+              + ["st%d" % j for j in range(N)] + ["mh0", "mh1"] + ["mx%d" % j for j in range(N)]
+              + ["sj%d" % j for j in range(N)] + ["tr%d" % j for j in range(6)]
+              + ["zi%d" % j for j in range(NB)] + ["bi%d" % j for j in range(NB)] + ["rl%d" % j for j in range(NB)])
 
 
 def rank_program(g, core, T, topo):
@@ -37,17 +44,16 @@ def rank_program(g, core, T, topo):
     n = len(cores)
     sem = T.sem
     te, ve = g.tensor, g.vector
+    amax = AluOpType.max
 
     def kslot(j):
-        return T.land[:, j * SLOT:j * SLOT + KP]
+        return T.kall[:, j * KP:(j + 1) * KP]
 
     def vslot(j):
-        return T.land[:, j * SLOT + KP:(j + 1) * SLOT]
-
-    own = T.land[:, rank * SLOT:(rank + 1) * SLOT]
+        return T.vall[:, j * KP:(j + 1) * KP]
 
     g.sync.dma_start(kslot(rank), T.k[:]).then_inc(sem.ldk, 16)
-    g.scalar.dma_start(vslot(rank), T.v[:]).then_inc(sem.ldv, 16)
+    g.sync.dma_start(vslot(rank), T.v[:]).then_inc(sem.ldv, 16)
     g.sync.dma_start(T.qs[:], T.q[:]).then_inc(sem.ldq, 16)
 
     dests = [(rank + i) % n for i in range(1, n)]
@@ -60,73 +66,109 @@ def rank_program(g, core, T, topo):
         rid, pid, _se = topo.addr(cores[d])
         ids.append(DstId(rid=rid, pnc=pid))
     g.wait_ge(sem.ldk, 16)
+    g.remote_dma_fused(
+        [RemoteDMATransfer(dst_ids=ids, dma_engine_mask=mask, remote_sem=sem["ka%d" % rank],
+                           srcs=[kslot(rank)], dsts=[kslot(rank) for _d in dests])],
+        local_sem=sem.sent)
     g.wait_ge(sem.ldv, 16)
     g.remote_dma_fused(
-        [RemoteDMATransfer(dst_ids=ids, dma_engine_mask=mask, remote_sem=sem["arr%d" % rank],
-                           srcs=[own], dsts=[own for _d in dests])],
+        [RemoteDMATransfer(dst_ids=ids, dma_engine_mask=mask, remote_sem=sem["va%d" % rank],
+                           srcs=[vslot(rank)], dsts=[vslot(rank) for _d in dests])],
         local_sem=sem.sent)
 
+    ve.memset(T.ones[0:1, :], 1.0).then_inc(sem.fillc, 1)
+    ve.memset(T.zrow[0:1, :], 0.0).then_inc(sem.fillc, 1)
+    ve.memset(T.zeros[:], 0.0).then_inc(sem.fillc, 1)
     ve.memset(T.stair[0:QP, :], 0.0).then_inc(sem.fill0, 1)
-    ve.memset(T.ones[0:1, :], 1.0).then_inc(sem.fill, 1)
-    ve.memset(T.zeros[:], 0.0).then_inc(sem.fill, 1)
     ve.wait_ge(sem.fill0, 1)
     for c in range(QP):
         ve.memset(T.stair[0:c + 1, c + 1:c + 2], -0.5).then_inc(sem.fill, 1)
-    ve.wait_ge(sem.fill, QP + 2)
-    ve.tensor_tensor(T.diag[0:QP, :], T.stair[0:QP, 1:QP + 1], T.stair[0:QP, 0:QP], AluOpType.subtract).then_inc(sem.idn, 1)
+    ve.wait_ge(sem.fill, QP)
+    ve.wait_ge(sem.fillc, 3)
+    for h in range(2):
+        ve.tensor_tensor(T.diag[0:QP, h * QP:(h + 1) * QP], T.stair[0:QP, 1:QP + 1], T.stair[0:QP, 0:QP],
+                         AluOpType.subtract).then_inc(sem.idn, 1)
 
     order = [rank] + [(rank - i) % n for i in range(1, n)]
-    st_ap = T.pm[0:QP, 0:KP]
+    width = [QP * len(order[2 * b:2 * b + 2]) for b in range(NB)]
+    te.wait_ge(sem.fillc, 3)
+    for b in range(NB):
+        te.matmul(T["sb%d" % b][:, 0:width[b]], T.ones[0:1, :], T.zrow[0:1, 0:width[b]], True, False).then_inc(sem["zi%d" % b], 1)
+
+    H = KP // 2
+    prev = None
     for i, j in enumerate(order):
+        b, h = i // 2, i % 2
+        tb = T["tb%d" % (i % NT)]
         if j == rank:
             te.wait_ge(sem.ldk, 16)
             te.wait_ge(sem.ldq, 16)
         else:
-            te.wait_ge(sem["arr%d" % j], eng)
-        if i > 0:
-            te.wait_ge(sem["mx%d" % (i - 1)], 1)
-        te.matmul(st_ap, T.qs[:], kslot(j), True, True).then_inc(sem["st%d" % i], 1)
-        te.matmul(T["ps%d" % j][:, 0:QP], kslot(j), T.qs[:], True, False)
+            te.wait_ge(sem["ka%d" % j], eng)
+        if i >= NT:
+            te.wait_ge(sem["mx%d" % (i - NT)], 1)
+        te.matmul(tb[0:QP, 0:KP], T.qs[:], kslot(j), True, True).then_inc(sem["st%d" % i], 1)
+        te.wait_ge(sem["zi%d" % b], 1)
+        te.matmul(T["sb%d" % b][:, h * QP:(h + 1) * QP], kslot(j), T.qs[:], False, False).then_inc(sem["sj%d" % i], 1)
         ve.wait_ge(sem["st%d" % i], 1)
-        blk = T.run[0:QP, i * KP:(i + 1) * KP]
         if i == 0:
-            ve.tensor_copy(blk, st_ap).then_inc(sem["mx%d" % i], 1)
+            e1 = T.run[0:QP, 0:KP]
+            ve.tensor_copy(e1, tb[0:QP, 0:KP]).then_inc(sem["mx%d" % i], 1)
+        elif i < n - 1:
+            e1 = T.run[0:QP, i * KP:(i + 1) * KP]
+            ve.tensor_tensor(e1, tb[0:QP, 0:KP], prev, amax).then_inc(sem["mx%d" % i], 1)
         else:
-            ve.wait_ge(sem["mx%d" % (i - 1)], 1)
-            ve.tensor_tensor(blk, st_ap, T.run[0:QP, (i - 1) * KP:i * KP], AluOpType.max).then_inc(sem["mx%d" % i], 1)
+            e0 = T.run[0:QP, i * KP + H:i * KP + 2 * H]
+            e1 = T.run[0:QP, i * KP + 2 * H:i * KP + 3 * H]
+            ve.tensor_tensor(e0, tb[0:QP, 0:H], prev, amax).then_inc(sem.mh1, 1)
+            ve.wait_ge(sem.mh1, 1)
+            ve.tensor_tensor(e1, tb[0:QP, H:KP], e0, amax).then_inc(sem["mx%d" % i], 1)
+        ve.wait_ge(sem["mx%d" % i], 1)
+        prev = e1
+        if i == n - 2:
+            f = T.run[0:QP, (i + 1) * KP:(i + 1) * KP + H]
+            ve.tensor_tensor(f, T.run[0:QP, i * KP:i * KP + H], T.run[0:QP, i * KP + H:(i + 1) * KP], amax).then_inc(sem.mh0, 1)
+            ve.wait_ge(sem.mh0, 1)
+            prev = f
 
-    ve.wait_ge(sem["mx%d" % (n - 1)], 1)
-    src, lo, w, off, step = T.run, (n - 1) * KP, KP // 2, 0, 0
+    src, lo, w = T.run, (n - 1) * KP + 2 * H, H // 2
+    off, step = 0, 0
     while w >= 1:
         out = T.tree[0:QP, off:off + w] if w > 1 else T.mcol[0:QP, 0:1]
-        ve.tensor_tensor(out, src[0:QP, lo:lo + w], src[0:QP, lo + w:lo + 2 * w], AluOpType.max).then_inc(sem["tr%d" % step], 1)
+        ve.tensor_tensor(out, src[0:QP, lo:lo + w], src[0:QP, lo + w:lo + 2 * w], amax).then_inc(sem["tr%d" % step], 1)
         ve.wait_ge(sem["tr%d" % step], 1)
         src, lo, off, w, step = T.tree, off, off + w, w // 2, step + 1
 
-    row_ap = T.pm[0:1, KP:KP + QP]
+    row_ap = T.pm[0:1, 0:2 * QP]
+    te.wait_ge(sem.idn, 2)
+    for i in range(n):
+        te.wait_ge(sem["sj%d" % i], 1)
     te.wait_ge(sem["tr%d" % (step - 1)], 1)
-    te.wait_ge(sem.idn, 1)
-    te.wait_ge(sem.fill, QP + 2)
     te.matmul(row_ap, T.mcol[0:QP, 0:1], T.diag[0:QP, :], True, True).then_inc(sem.row, 1)
     ve.wait_ge(sem.row, 1)
     ve.tensor_copy(T.mrow[0:1, :], row_ap).then_inc(sem.mr, 1)
     te.wait_ge(sem.mr, 1)
-    for j in order:
-        te.matmul(T["ps%d" % j][:, 0:QP], T.ones[0:1, :], T.mrow[0:1, :], False, True).then_inc(sem["bi%d" % j], 1)
-    for j in order:
-        ve.wait_ge(sem["bi%d" % j], 1)
-        ve.tensor_tensor(T.p[:, j * QP:(j + 1) * QP], T["ps%d" % j][:, 0:QP], T.zeros[:], AluOpType.max).then_inc(sem["rl%d" % j], 1)
+    for b in range(NB):
+        te.matmul(T["sb%d" % b][:, 0:width[b]], T.ones[0:1, :], T.mrow[0:1, 0:width[b]], False, True).then_inc(sem["bi%d" % b], 1)
+    for b in range(NB):
+        ve.wait_ge(sem["bi%d" % b], 1)
+        ve.tensor_tensor(T.p[:, 2 * b * QP:2 * b * QP + width[b]], T["sb%d" % b][:, 0:width[b]], T.zeros[:, 0:width[b]],
+                         amax).then_inc(sem["rl%d" % b], 1)
 
-    y_ap = T.pm[:, 2 * KP:2 * KP + QP]
-    te.wait_ge(sem.ldv, 16)
+    y_ap = T.pm[:, KP:KP + QP]
     last = None
     for i, j in enumerate(order):
-        te.wait_ge(sem["rl%d" % j], 1)
-        last = te.matmul(y_ap, vslot(j), T.p[:, j * QP:(j + 1) * QP], i == 0, i == n - 1)
+        if i % 2 == 0:
+            te.wait_ge(sem["rl%d" % (i // 2)], 1)
+        if j == rank:
+            te.wait_ge(sem.ldv, 16)
+        else:
+            te.wait_ge(sem["va%d" % j], eng)
+        last = te.matmul(y_ap, vslot(j), T.p[:, i * QP:(i + 1) * QP], i == 0, i == n - 1)
     last.then_inc(sem.yd, 1)
     ve.wait_ge(sem.yd, 1)
     ve.tensor_copy(T.ysb[:], y_ap).then_inc(sem.yc, 1)
     g.sync.wait_ge(sem.yc, 1)
     g.sync.dma_start(T.y[:], T.ysb[:]).then_inc(sem.stored, 16)
     g.sync.wait_ge(sem.stored, 16)
-    g.wait_ge(sem.sent, eng)
+    g.wait_ge(sem.sent, 2 * eng)

@@ -1,39 +1,94 @@
 from concourse.bass import DstId, RemoteDMATransfer
-from concourse.mybir import dt, AluOpType
+from concourse.mybir import dt, AluOpType, AxisListType
 
 N = 7
 QP = 32
 KP = 128
-NB = (N + 1) // 2
-NT = 3
+G = KP // QP
+NBL = 4
+ZW = 96
 
 SCRATCH = {
     "kall": ("sbuf", [128, N * KP], "bfloat16"),
     "vall": ("sbuf", [128, N * KP], "bfloat16"),
     "qs": ("sbuf", [128, QP], "bfloat16"),
     "stair": ("sbuf", [128, QP + 1], "bfloat16"),
-    "diag": ("sbuf", [128, 2 * QP], "bfloat16"),
-    "ones": ("sbuf", [128, KP], "bfloat16"),
-    "zrow": ("sbuf", [128, 2 * QP], "bfloat16"),
-    "zeros": ("sbuf", [128, 2 * QP], "float32"),
-    "run": ("sbuf", [128, 2 * N * KP], "float32"),
-    "tree": ("sbuf", [128, KP], "float32"),
-    "mcol": ("sbuf", [128, 8], "bfloat16"),
-    "mrow": ("sbuf", [128, 2 * QP], "bfloat16"),
-    "p": ("sbuf", [128, 2 * NB * QP], "bfloat16"),
+    "eye": ("sbuf", [128, KP], "bfloat16"),
+    "rep": ("sbuf", [128, KP], "bfloat16"),
+    "mk": ("sbuf", [128, G], "float32"),
+    "zt": ("sbuf", [128, NBL * ZW], "float32"),
+    "zm": ("sbuf", [128, 4], "float32"),
+    "r4": ("sbuf", [128, 8], "bfloat16"),
+    "nh": ("sbuf", [128, 4], "float32"),
+    "pt": ("sbuf", [128, N * QP], "bfloat16"),
+    "p": ("sbuf", [128, N * QP], "bfloat16"),
     "ysb": ("sbuf", [128, QP], "bfloat16"),
     "pm": ("psum", [128, 512], "float32"),
+    "rp": ("psum", [128, 512], "float32"),
+    "cb": ("psum", [128, 512], "float32"),
 }
-for _j in range(NB):
-    SCRATCH["sb%d" % _j] = ("psum", [128, 512], "float32")
-for _j in range(NT):
-    SCRATCH["tb%d" % _j] = ("psum", [128, 512], "float32")
+for _b in range(NBL):
+    SCRATCH["sb%d" % _b] = ("psum", [128, 512], "float32")
 
-SEMAPHORES = (["ldk", "ldv", "ldq", "sent", "stored", "fillc", "fill0", "fill", "idn", "row", "mr", "yd", "yc"]
+SEMAPHORES = (["ldk", "ldv", "ldq", "sent", "stored", "fill0", "fill", "idn", "mk0", "mk1", "rpm", "reps",
+               "r4s", "cbs", "nhs", "yd", "yc"]
               + ["ka%d" % j for j in range(N)] + ["va%d" % j for j in range(N)]
-              + ["st%d" % j for j in range(N)] + ["mh0", "mh1"] + ["mx%d" % j for j in range(N)]
-              + ["sj%d" % j for j in range(N)] + ["tr%d" % j for j in range(6)]
-              + ["zi%d" % j for j in range(NB)] + ["bi%d" % j for j in range(NB)] + ["rl%d" % j for j in range(NB)])
+              + ["sj%d" % j for j in range(NBL)] + ["zs%d" % j for j in range(NBL)] + ["mx%d" % j for j in range(NBL)]
+              + ["ts%d" % j for j in range(NBL)] + ["tr%d" % j for j in range(NBL)])
+
+_CACHE = {}
+
+
+def _way(topo, s, d):
+    cs, cd, di = topo.chip(s), topo.chip(d), topo.die(s)
+    if cs == cd:
+        return ()
+    if topo.same_plane(cs, cd):
+        return (("out", cs, di), ("in", cd, di))
+    if topo.mates(cs, cd):
+        return (("mate", cs, di),)
+    m = [c for c in range(topo.CHIPS) if topo.mates(cs, c)][0]
+    return (("mate", cs, di), ("out", m, di), ("in", cd, di))
+
+
+def _rounds(topo, cores):
+    key = tuple(cores)
+    if key not in _CACHE:
+        n = len(cores)
+        way = {(a, b): _way(topo, cores[a], cores[b]) for a in range(n) for b in range(n) if a != b}
+        good = [[] for _d in range(n)]
+        perm = [0] * n
+
+        def fill(r, taken, busy):
+            if r == n:
+                bits = 0
+                for a in range(n):
+                    bits |= 1 << (a * n + perm[a])
+                good[perm[0]].append((bits, tuple(perm)))
+                return
+            for d in range(n):
+                if d == r or d in taken or any(l in busy for l in way[(r, d)]):
+                    continue
+                perm[r] = d
+                fill(r + 1, taken | {d}, busy | set(way[(r, d)]))
+
+        def cover(d0, bits, chosen):
+            if d0 == n:
+                return chosen
+            for b, p in good[d0]:
+                if b & bits:
+                    continue
+                res = cover(d0 + 1, bits | b, chosen + [p])
+                if res is not None:
+                    return res
+            return None
+
+        fill(0, frozenset(), frozenset())
+        found = cover(1, 0, [])
+        if found is None:
+            found = [tuple((r + s) % n for r in range(n)) for s in range(1, n)]
+        _CACHE[key] = found
+    return _CACHE[key]
 
 
 def rank_program(g, core, T, topo):
@@ -44,7 +99,6 @@ def rank_program(g, core, T, topo):
     n = len(cores)
     sem = T.sem
     te, ve = g.tensor, g.vector
-    amax = AluOpType.max
 
     def kslot(j):
         return T.kall[:, j * KP:(j + 1) * KP]
@@ -53,10 +107,11 @@ def rank_program(g, core, T, topo):
         return T.vall[:, j * KP:(j + 1) * KP]
 
     g.sync.dma_start(kslot(rank), T.k[:]).then_inc(sem.ldk, 16)
-    g.sync.dma_start(vslot(rank), T.v[:]).then_inc(sem.ldv, 16)
+    g.scalar.dma_start(vslot(rank), T.v[:]).then_inc(sem.ldv, 16)
     g.sync.dma_start(T.qs[:], T.q[:]).then_inc(sem.ldq, 16)
 
-    dests = [(rank + i) % n for i in range(1, n)]
+    rounds = _rounds(topo, list(cores))
+    dests = [rd[rank] for rd in rounds]
     mask = topo.mask(core, cores[dests[0]])
     for d in dests:
         mask &= topo.mask(core, cores[d])
@@ -76,95 +131,83 @@ def rank_program(g, core, T, topo):
                            srcs=[vslot(rank)], dsts=[vslot(rank) for _d in dests])],
         local_sem=sem.sent)
 
-    ve.memset(T.ones[0:1, :], 1.0).then_inc(sem.fillc, 1)
-    ve.memset(T.zrow[0:1, :], 0.0).then_inc(sem.fillc, 1)
-    ve.memset(T.zeros[:], 0.0).then_inc(sem.fillc, 1)
     ve.memset(T.stair[0:QP, :], 0.0).then_inc(sem.fill0, 1)
+    ve.memset(T.mk[:, :], 0.0).then_inc(sem.mk0, 1)
     ve.wait_ge(sem.fill0, 1)
     for c in range(QP):
-        ve.memset(T.stair[0:c + 1, c + 1:c + 2], -0.5).then_inc(sem.fill, 1)
+        ve.memset(T.stair[0:c + 1, c + 1:c + 2], 1.0).then_inc(sem.fill, 1)
     ve.wait_ge(sem.fill, QP)
-    ve.wait_ge(sem.fillc, 3)
-    for h in range(2):
-        ve.tensor_tensor(T.diag[0:QP, h * QP:(h + 1) * QP], T.stair[0:QP, 1:QP + 1], T.stair[0:QP, 0:QP],
+    for a in range(G):
+        ve.tensor_tensor(T.eye[0:QP, a * QP:(a + 1) * QP], T.stair[0:QP, 1:QP + 1], T.stair[0:QP, 0:QP],
                          AluOpType.subtract).then_inc(sem.idn, 1)
+    ve.wait_ge(sem.mk0, 1)
+    for a in range(G):
+        ve.memset(T.mk[a * QP:(a + 1) * QP, a:a + 1], 1.0).then_inc(sem.mk1, 1)
+    te.wait_ge(sem.idn, G)
+    te.matmul(T.rp[:, 0:KP], T.eye[0:QP, :], T.eye[0:QP, :], True, True).then_inc(sem.rpm, 1)
+    ve.wait_ge(sem.rpm, 1)
+    ve.tensor_scalar(T.rep[:, :], T.rp[:, 0:KP], -0.5, None, AluOpType.mult).then_inc(sem.reps, 1)
+    ve.wait_ge(sem.mk1, G)
 
-    order = [rank] + [(rank - i) % n for i in range(1, n)]
-    width = [QP * len(order[2 * b:2 * b + 2]) for b in range(NB)]
-    te.wait_ge(sem.fillc, 3)
-    for b in range(NB):
-        te.matmul(T["sb%d" % b][:, 0:width[b]], T.ones[0:1, :], T.zrow[0:1, 0:width[b]], True, False).then_inc(sem["zi%d" % b], 1)
-
-    H = KP // 2
-    prev = None
-    for i, j in enumerate(order):
-        b, h = i // 2, i % 2
-        tb = T["tb%d" % (i % NT)]
-        if j == rank:
-            te.wait_ge(sem.ldk, 16)
-            te.wait_ge(sem.ldq, 16)
+    order = [rank] + [list(rd).index(rank) for rd in rounds]
+    blocks = [(0, 1)] + [(lo, lo + 2) for lo in range(1, n, 2)]
+    for b, (lo, hi) in enumerate(blocks):
+        sb = T["sb%d" % b]
+        w = (hi - lo) * QP
+        for i in range(lo, hi):
+            j = order[i]
+            if i == 0:
+                te.wait_ge(sem.ldk, 16)
+                te.wait_ge(sem.ldq, 16)
+            else:
+                te.wait_ge(sem["ka%d" % j], eng)
+            te.matmul(sb[:, (i - lo) * QP:(i - lo + 1) * QP], kslot(j), T.qs[:], True, True).then_inc(sem["sj%d" % b], 1)
+        ve.wait_ge(sem["sj%d" % b], hi - lo)
+        ve.transpose(T.zt[:, b * ZW:b * ZW + w], sb[:, 0:w]).then_inc(sem["zs%d" % b], 1)
+        ve.wait_ge(sem["zs%d" % b], 1)
+        if b > 0:
+            ve.wait_ge(sem["mx%d" % (b - 1)], 1)
+        wr = w if b == 0 else w + 1
+        if b < len(blocks) - 1:
+            nlo, nhi = blocks[b + 1]
+            col = (b + 1) * ZW + (nhi - nlo) * QP
+            out = T.zt[:, col:col + 1]
         else:
-            te.wait_ge(sem["ka%d" % j], eng)
-        if i >= NT:
-            te.wait_ge(sem["mx%d" % (i - NT)], 1)
-        te.matmul(tb[0:QP, 0:KP], T.qs[:], kslot(j), True, True).then_inc(sem["st%d" % i], 1)
-        te.wait_ge(sem["zi%d" % b], 1)
-        te.matmul(T["sb%d" % b][:, h * QP:(h + 1) * QP], kslot(j), T.qs[:], False, False).then_inc(sem["sj%d" % i], 1)
-        ve.wait_ge(sem["st%d" % i], 1)
-        if i == 0:
-            e1 = T.run[0:QP, 0:KP]
-            ve.tensor_copy(e1, tb[0:QP, 0:KP]).then_inc(sem["mx%d" % i], 1)
-        elif i < n - 1:
-            e1 = T.run[0:QP, i * KP:(i + 1) * KP]
-            ve.tensor_tensor(e1, tb[0:QP, 0:KP], prev, amax).then_inc(sem["mx%d" % i], 1)
-        else:
-            e0 = T.run[0:QP, i * KP + H:i * KP + 2 * H]
-            e1 = T.run[0:QP, i * KP + 2 * H:i * KP + 3 * H]
-            ve.tensor_tensor(e0, tb[0:QP, 0:H], prev, amax).then_inc(sem.mh1, 1)
-            ve.wait_ge(sem.mh1, 1)
-            ve.tensor_tensor(e1, tb[0:QP, H:KP], e0, amax).then_inc(sem["mx%d" % i], 1)
-        ve.wait_ge(sem["mx%d" % i], 1)
-        prev = e1
-        if i == n - 2:
-            f = T.run[0:QP, (i + 1) * KP:(i + 1) * KP + H]
-            ve.tensor_tensor(f, T.run[0:QP, i * KP:i * KP + H], T.run[0:QP, i * KP + H:(i + 1) * KP], amax).then_inc(sem.mh0, 1)
-            ve.wait_ge(sem.mh0, 1)
-            prev = f
+            out = T.zm[:, 0:1]
+        ve.tensor_reduce(out, T.zt[:, b * ZW:b * ZW + wr], AxisListType.X, AluOpType.max).then_inc(sem["mx%d" % b], 1)
 
-    src, lo, w = T.run, (n - 1) * KP + 2 * H, H // 2
-    off, step = 0, 0
-    while w >= 1:
-        out = T.tree[0:QP, off:off + w] if w > 1 else T.mcol[0:QP, 0:1]
-        ve.tensor_tensor(out, src[0:QP, lo:lo + w], src[0:QP, lo + w:lo + 2 * w], amax).then_inc(sem["tr%d" % step], 1)
-        ve.wait_ge(sem["tr%d" % step], 1)
-        src, lo, off, w, step = T.tree, off, off + w, w // 2, step + 1
+    nb = len(blocks)
+    ve.wait_ge(sem["mx%d" % (nb - 1)], 1)
+    ve.tensor_scalar(T.r4[:, 0:G], T.mk[:, :], T.zm[:, 0:1], None, AluOpType.mult).then_inc(sem.r4s, 1)
+    te.wait_ge(sem.reps, 1)
+    te.wait_ge(sem.r4s, 1)
+    te.matmul(T.cb[:, 0:G], T.rep[:, :], T.r4[:, 0:G], True, True).then_inc(sem.cbs, 1)
+    ve.wait_ge(sem.cbs, 1)
+    ve.tensor_reduce(T.nh[:, 0:1], T.cb[:, 0:G], AxisListType.X, AluOpType.min).then_inc(sem.nhs, 1)
+    ve.wait_ge(sem.nhs, 1)
 
-    row_ap = T.pm[0:1, 0:2 * QP]
-    te.wait_ge(sem.idn, 2)
-    for i in range(n):
-        te.wait_ge(sem["sj%d" % i], 1)
-    te.wait_ge(sem["tr%d" % (step - 1)], 1)
-    te.matmul(row_ap, T.mcol[0:QP, 0:1], T.diag[0:QP, :], True, True).then_inc(sem.row, 1)
-    ve.wait_ge(sem.row, 1)
-    ve.tensor_copy(T.mrow[0:1, :], row_ap).then_inc(sem.mr, 1)
-    te.wait_ge(sem.mr, 1)
-    for b in range(NB):
-        te.matmul(T["sb%d" % b][:, 0:width[b]], T.ones[0:1, :], T.mrow[0:1, 0:width[b]], False, True).then_inc(sem["bi%d" % b], 1)
-    for b in range(NB):
-        ve.wait_ge(sem["bi%d" % b], 1)
-        ve.tensor_tensor(T.p[:, 2 * b * QP:2 * b * QP + width[b]], T["sb%d" % b][:, 0:width[b]], T.zeros[:, 0:width[b]],
-                         amax).then_inc(sem["rl%d" % b], 1)
+    turn = list(range(1, nb)) + [0]
+    for b in turn:
+        lo, hi = blocks[b]
+        w = (hi - lo) * QP
+        ve.tensor_scalar(T.pt[:, lo * QP:hi * QP], T.zt[:, b * ZW:b * ZW + w], T.nh[:, 0:1], 0.0,
+                         AluOpType.add, AluOpType.max).then_inc(sem["ts%d" % b], 1)
+        ve.wait_ge(sem["ts%d" % b], 1)
+        ve.transpose(T.p[:, lo * QP:hi * QP], T.pt[:, lo * QP:hi * QP]).then_inc(sem["tr%d" % b], 1)
 
-    y_ap = T.pm[:, KP:KP + QP]
+    y_ap = T.pm[:, 0:QP]
+    seq = [i for b in turn for i in range(blocks[b][0], blocks[b][1])]
     last = None
-    for i, j in enumerate(order):
-        if i % 2 == 0:
-            te.wait_ge(sem["rl%d" % (i // 2)], 1)
+    for c, i in enumerate(seq):
+        j = order[i]
+        for b in turn:
+            if blocks[b][0] == i:
+                te.wait_ge(sem["tr%d" % b], 1)
         if j == rank:
             te.wait_ge(sem.ldv, 16)
         else:
             te.wait_ge(sem["va%d" % j], eng)
-        last = te.matmul(y_ap, vslot(j), T.p[:, i * QP:(i + 1) * QP], i == 0, i == n - 1)
+        last = te.matmul(y_ap, vslot(j), T.p[:, i * QP:(i + 1) * QP], c == 0, c == n - 1)
     last.then_inc(sem.yd, 1)
     ve.wait_ge(sem.yd, 1)
     ve.tensor_copy(T.ysb[:], y_ap).then_inc(sem.yc, 1)

@@ -1,40 +1,35 @@
 from concourse.bass import DstId, RemoteDMATransfer
-from concourse.mybir import dt, AluOpType, AxisListType
+from concourse.mybir import dt, AluOpType, AxisListType, ActivationFunctionType
 
 N = 7
 QP = 32
 KP = 128
-G = KP // QP
-NBL = 4
-ZW = 96
+GROUPS = [(0, 3), (3, 5), (5, 6), (6, 7)]
+NA = 4
 
 SCRATCH = {
     "kall": ("sbuf", [128, N * KP], "bfloat16"),
     "vall": ("sbuf", [128, N * KP], "bfloat16"),
     "qs": ("sbuf", [128, QP], "bfloat16"),
+    "zb": ("sbuf", [128, KP], "bfloat16"),
     "stair": ("sbuf", [128, QP + 1], "bfloat16"),
     "eye": ("sbuf", [128, KP], "bfloat16"),
-    "rep": ("sbuf", [128, KP], "bfloat16"),
-    "mk": ("sbuf", [128, G], "float32"),
-    "zt": ("sbuf", [128, NBL * ZW], "float32"),
-    "zm": ("sbuf", [128, 4], "float32"),
-    "r4": ("sbuf", [128, 8], "bfloat16"),
-    "nh": ("sbuf", [128, 4], "float32"),
-    "pt": ("sbuf", [128, N * QP], "bfloat16"),
+    "mx": ("sbuf", [128, 4], "float32"),
+    "bb": ("sbuf", [128, KP], "bfloat16"),
+    "ml": ("sbuf", [128, KP], "bfloat16"),
     "p": ("sbuf", [128, N * QP], "bfloat16"),
     "ysb": ("sbuf", [128, QP], "bfloat16"),
     "pm": ("psum", [128, 512], "float32"),
-    "rp": ("psum", [128, 512], "float32"),
-    "cb": ("psum", [128, 512], "float32"),
+    "sa": ("psum", [128, 512], "float32"),
+    "sb": ("psum", [128, 512], "float32"),
 }
-for _b in range(NBL):
-    SCRATCH["sb%d" % _b] = ("psum", [128, 512], "float32")
+for _b in range(len(GROUPS)):
+    SCRATCH["t%d" % _b] = ("psum", [128, 512], "float32")
 
-SEMAPHORES = (["ldk", "ldv", "ldq", "sent", "stored", "fill0", "fill", "idn", "mk0", "mk1", "rpm", "reps",
-               "r4s", "cbs", "nhs", "yd", "yc"]
+SEMAPHORES = (["ldk", "ldv", "ldq", "sent", "vh", "stored", "zs", "fill0", "fill", "idn", "gz", "ga", "gb",
+               "bs", "mls", "ba", "bbs", "pa0", "pa1", "pb", "yd", "yc"]
               + ["ka%d" % j for j in range(N)] + ["va%d" % j for j in range(N)]
-              + ["sj%d" % j for j in range(NBL)] + ["zs%d" % j for j in range(NBL)] + ["mx%d" % j for j in range(NBL)]
-              + ["ts%d" % j for j in range(NBL)] + ["tr%d" % j for j in range(NBL)])
+              + ["st%d" % j for j in range(len(GROUPS))] + ["rd%d" % j for j in range(len(GROUPS))])
 
 _CACHE = {}
 
@@ -91,14 +86,51 @@ def _rounds(topo, cores):
     return _CACHE[key]
 
 
+def _plan(topo, cores, rounds, r):
+    core = cores[r]
+    dests = [rd[r] for rd in rounds]
+    cand = [c for c in range(topo.CHIPS * topo.CORES_PER_CHIP)
+            if topo.chip(c) == topo.chip(core) and c not in cores and topo.die(c) != topo.die(core)
+            and all(topo.may_write(c, cores[d]) for d in dests)]
+    if len(cand) < 2 or len(dests) != 6:
+        return dests, []
+    return dests[0:2], [(cand[0], dests[2:4]), (cand[1], dests[4:6])]
+
+
+def _mask(topo, src, dsts):
+    m = topo.mask(src, dsts[0])
+    for d in dsts:
+        m &= topo.mask(src, d)
+    return m
+
+
+def _bits(m):
+    return bin(m).count("1")
+
+
+def _ids(topo, dsts):
+    out = []
+    for d in dsts:
+        rid, pid, _se = topo.addr(d)
+        out.append(DstId(rid=rid, pnc=pid))
+    return out
+
+
+def _chip_mask(topo, cores, rounds, r):
+    core = cores[r]
+    _direct, helpers = _plan(topo, cores, rounds, r)
+    on = _mask(topo, core, [h for h, _ds in helpers])
+    off = _mask(topo, core, [cores[rd[r]] for rd in rounds])
+    free = on & ~off
+    return free if _bits(free) in (1, 2, 4, 8, 16) else on
+
+
 def rank_program(g, core, T, topo):
-    rank = T.rank_of(core)
-    if rank is None:
-        return
-    cores = T.cores
+    cores = list(T.cores)
     n = len(cores)
     sem = T.sem
-    te, ve = g.tensor, g.vector
+    rounds = _rounds(topo, cores)
+    rank = T.rank_of(core)
 
     def kslot(j):
         return T.kall[:, j * KP:(j + 1) * KP]
@@ -106,54 +138,86 @@ def rank_program(g, core, T, topo):
     def vslot(j):
         return T.vall[:, j * KP:(j + 1) * KP]
 
+    if rank is None:
+        for r in range(n):
+            _direct, helpers = _plan(topo, cores, rounds, r)
+            for h, ds in helpers:
+                if h != core:
+                    continue
+                hm = _mask(topo, core, [cores[d] for d in ds])
+                g.wait_ge(sem.vh, _bits(_chip_mask(topo, cores, rounds, r)))
+                g.remote_dma_fused(
+                    [RemoteDMATransfer(dst_ids=_ids(topo, [cores[d] for d in ds]), dma_engine_mask=hm,
+                                       remote_sem=sem["va%d" % r], srcs=[vslot(r)], dsts=[vslot(r) for _d in ds])],
+                    local_sem=sem.sent)
+                g.wait_ge(sem.sent, _bits(hm))
+        return
+
+    te, ve = g.tensor, g.vector
+
     g.sync.dma_start(kslot(rank), T.k[:]).then_inc(sem.ldk, 16)
     g.scalar.dma_start(vslot(rank), T.v[:]).then_inc(sem.ldv, 16)
     g.sync.dma_start(T.qs[:], T.q[:]).then_inc(sem.ldq, 16)
 
-    rounds = _rounds(topo, list(cores))
     dests = [rd[rank] for rd in rounds]
-    mask = topo.mask(core, cores[dests[0]])
-    for d in dests:
-        mask &= topo.mask(core, cores[d])
-    eng = bin(mask).count("1")
-    ids = []
-    for d in dests:
-        rid, pid, _se = topo.addr(cores[d])
-        ids.append(DstId(rid=rid, pnc=pid))
+    mask = _mask(topo, core, [cores[d] for d in dests])
+    eng = _bits(mask)
+    direct, helpers = _plan(topo, cores, rounds, rank)
+    sent = 0
     g.wait_ge(sem.ldk, 16)
     g.remote_dma_fused(
-        [RemoteDMATransfer(dst_ids=ids, dma_engine_mask=mask, remote_sem=sem["ka%d" % rank],
-                           srcs=[kslot(rank)], dsts=[kslot(rank) for _d in dests])],
+        [RemoteDMATransfer(dst_ids=_ids(topo, [cores[d] for d in dests]), dma_engine_mask=mask,
+                           remote_sem=sem["ka%d" % rank], srcs=[kslot(rank)], dsts=[kslot(rank) for _d in dests])],
         local_sem=sem.sent)
+    sent += eng
     g.wait_ge(sem.ldv, 16)
+    if helpers:
+        cm = _chip_mask(topo, cores, rounds, rank)
+        g.remote_dma_fused(
+            [RemoteDMATransfer(dst_ids=_ids(topo, [h for h, _ds in helpers]), dma_engine_mask=cm,
+                               remote_sem=sem.vh, srcs=[vslot(rank)], dsts=[vslot(rank) for _h in helpers])],
+            local_sem=sem.sent)
+        sent += _bits(cm)
     g.remote_dma_fused(
-        [RemoteDMATransfer(dst_ids=ids, dma_engine_mask=mask, remote_sem=sem["va%d" % rank],
-                           srcs=[vslot(rank)], dsts=[vslot(rank) for _d in dests])],
+        [RemoteDMATransfer(dst_ids=_ids(topo, [cores[d] for d in direct]), dma_engine_mask=mask,
+                           remote_sem=sem["va%d" % rank], srcs=[vslot(rank)], dsts=[vslot(rank) for _d in direct])],
         local_sem=sem.sent)
+    sent += eng
 
+    def v_count(j):
+        dj, hj = _plan(topo, cores, rounds, j)
+        for h, ds in hj:
+            if rank in ds:
+                return _bits(_mask(topo, h, [cores[d] for d in ds])), False
+        return _bits(_mask(topo, cores[j], [cores[rd[j]] for rd in rounds])), True
+
+    ve.memset(T.zb[0:QP, :], 0.0).then_inc(sem.zs, 1)
     ve.memset(T.stair[0:QP, :], 0.0).then_inc(sem.fill0, 1)
-    ve.memset(T.mk[:, :], 0.0).then_inc(sem.mk0, 1)
     ve.wait_ge(sem.fill0, 1)
     for c in range(QP):
-        ve.memset(T.stair[0:c + 1, c + 1:c + 2], 1.0).then_inc(sem.fill, 1)
+        ve.memset(T.stair[0:c + 1, c + 1:c + 2], -0.5).then_inc(sem.fill, 1)
     ve.wait_ge(sem.fill, QP)
-    for a in range(G):
+    for a in range(KP // QP):
         ve.tensor_tensor(T.eye[0:QP, a * QP:(a + 1) * QP], T.stair[0:QP, 1:QP + 1], T.stair[0:QP, 0:QP],
                          AluOpType.subtract).then_inc(sem.idn, 1)
-    ve.wait_ge(sem.mk0, 1)
-    for a in range(G):
-        ve.memset(T.mk[a * QP:(a + 1) * QP, a:a + 1], 1.0).then_inc(sem.mk1, 1)
-    te.wait_ge(sem.idn, G)
-    te.matmul(T.rp[:, 0:KP], T.eye[0:QP, :], T.eye[0:QP, :], True, True).then_inc(sem.rpm, 1)
-    ve.wait_ge(sem.rpm, 1)
-    ve.tensor_scalar(T.rep[:, :], T.rp[:, 0:KP], -0.5, None, AluOpType.mult).then_inc(sem.reps, 1)
-    ve.wait_ge(sem.mk1, G)
 
     order = [rank] + [list(rd).index(rank) for rd in rounds]
-    blocks = [(0, 1)] + [(lo, lo + 2) for lo in range(1, n, 2)]
-    for b, (lo, hi) in enumerate(blocks):
-        sb = T["sb%d" % b]
-        w = (hi - lo) * QP
+    late = [i for i in range(1, n) if v_count(order[i])[1]]
+    seq = [0] + [i for i in range(1, n) if i not in late] + late
+    slot = {i: s for s, i in enumerate(seq)}
+    wa, wb = NA * QP, (n - NA) * QP
+
+    def s_ap(i):
+        s = slot[i]
+        return T.sa[:, s * QP:(s + 1) * QP] if s < NA else T.sb[:, (s - NA) * QP:(s - NA + 1) * QP]
+
+    te.wait_ge(sem.zs, 1)
+    te.matmul(T.sa[:, 0:wa], T.zb[0:QP, :], T.zb[0:QP, 0:wa], True, False).then_inc(sem.gz, 1)
+    te.matmul(T.sb[:, 0:wb], T.zb[0:QP, :], T.zb[0:QP, 0:wb], True, False).then_inc(sem.gz, 1)
+    te.wait_ge(sem.gz, 2)
+
+    for b, (lo, hi) in enumerate(GROUPS):
+        tb = T["t%d" % b]
         for i in range(lo, hi):
             j = order[i]
             if i == 0:
@@ -161,57 +225,64 @@ def rank_program(g, core, T, topo):
                 te.wait_ge(sem.ldq, 16)
             else:
                 te.wait_ge(sem["ka%d" % j], eng)
-            te.matmul(sb[:, (i - lo) * QP:(i - lo + 1) * QP], kslot(j), T.qs[:], True, True).then_inc(sem["sj%d" % b], 1)
-        ve.wait_ge(sem["sj%d" % b], hi - lo)
-        ve.transpose(T.zt[:, b * ZW:b * ZW + w], sb[:, 0:w]).then_inc(sem["zs%d" % b], 1)
-        ve.wait_ge(sem["zs%d" % b], 1)
-        if b > 0:
-            ve.wait_ge(sem["mx%d" % (b - 1)], 1)
-        wr = w if b == 0 else w + 1
-        if b < len(blocks) - 1:
-            nlo, nhi = blocks[b + 1]
-            col = (b + 1) * ZW + (nhi - nlo) * QP
-            out = T.zt[:, col:col + 1]
-        else:
-            out = T.zm[:, 0:1]
-        ve.tensor_reduce(out, T.zt[:, b * ZW:b * ZW + wr], AxisListType.X, AluOpType.max).then_inc(sem["mx%d" % b], 1)
+            te.matmul(tb[0:QP, (i - lo) * KP:(i - lo + 1) * KP], T.qs[:], kslot(j), True, True).then_inc(
+                sem["st%d" % b], 1)
+            te.matmul(s_ap(i), kslot(j), T.qs[:], False, False).then_inc(sem.ga if slot[i] < NA else sem.gb, 1)
 
-    nb = len(blocks)
-    ve.wait_ge(sem["mx%d" % (nb - 1)], 1)
-    ve.tensor_scalar(T.r4[:, 0:G], T.mk[:, :], T.zm[:, 0:1], None, AluOpType.mult).then_inc(sem.r4s, 1)
-    te.wait_ge(sem.reps, 1)
-    te.wait_ge(sem.r4s, 1)
-    te.matmul(T.cb[:, 0:G], T.rep[:, :], T.r4[:, 0:G], True, True).then_inc(sem.cbs, 1)
-    ve.wait_ge(sem.cbs, 1)
-    ve.tensor_reduce(T.nh[:, 0:1], T.cb[:, 0:G], AxisListType.X, AluOpType.min).then_inc(sem.nhs, 1)
-    ve.wait_ge(sem.nhs, 1)
+    def reduce(b):
+        lo, hi = GROUPS[b]
+        ve.wait_ge(sem["st%d" % b], hi - lo)
+        ve.tensor_reduce(T.mx[0:QP, b:b + 1], T["t%d" % b][0:QP, 0:(hi - lo) * KP], AxisListType.X,
+                         AluOpType.max).then_inc(sem["rd%d" % b], 1)
 
-    turn = list(range(1, nb)) + [0]
-    for b in turn:
-        lo, hi = blocks[b]
-        w = (hi - lo) * QP
-        ve.tensor_scalar(T.pt[:, lo * QP:hi * QP], T.zt[:, b * ZW:b * ZW + w], T.nh[:, 0:1], 0.0,
-                         AluOpType.add, AluOpType.max).then_inc(sem["ts%d" % b], 1)
-        ve.wait_ge(sem["ts%d" % b], 1)
-        ve.transpose(T.p[:, lo * QP:hi * QP], T.pt[:, lo * QP:hi * QP]).then_inc(sem["tr%d" % b], 1)
+    reduce(0)
+    reduce(1)
+    reduce(2)
+    ve.wait_ge(sem.zs, 1)
+    ve.wait_ge(sem.rd0, 1)
+    ve.wait_ge(sem.rd1, 1)
+    ve.tensor_scalar(T.bb[0:QP, :], T.zb[0:QP, :], T.mx[0:QP, 0:1], T.mx[0:QP, 1:2],
+                     AluOpType.add, AluOpType.max).then_inc(sem.bs, 1)
+    reduce(3)
+    ve.wait_ge(sem.bs, 1)
+    ve.wait_ge(sem.rd2, 1)
+    ve.wait_ge(sem.rd3, 1)
+    ve.tensor_scalar(T.ml[0:QP, :], T.bb[0:QP, :], T.mx[0:QP, 2:3], T.mx[0:QP, 3:4],
+                     AluOpType.max, AluOpType.max).then_inc(sem.mls, 1)
+
+    te.wait_ge(sem.idn, KP // QP)
+    te.wait_ge(sem.ga, NA)
+    te.wait_ge(sem.gb, n - NA)
+    te.wait_ge(sem.mls, 1)
+    te.matmul(T.sa[:, 0:wa], T.ml[0:QP, :], T.eye[0:QP, 0:wa], False, True).then_inc(sem.ba, 1)
+    te.matmul(T.sb[:, 0:wb], T.ml[0:QP, :], T.eye[0:QP, 0:wb], False, True).then_inc(sem.bbs, 1)
+
+    ve.wait_ge(sem.ba, 1)
+    ha = wa // 2
+    ve.tensor_scalar(T.p[:, 0:ha], T.sa[:, 0:ha], 0.0, None, AluOpType.max).then_inc(sem.pa0, 1)
+    ve.tensor_scalar(T.p[:, ha:wa], T.sa[:, ha:wa], 0.0, None, AluOpType.max).then_inc(sem.pa1, 1)
+    g.scalar.wait_ge(sem.bbs, 1)
+    g.scalar.activation(T.p[:, wa:wa + wb], T.sb[:, 0:wb], ActivationFunctionType.Relu).then_inc(sem.pb, 1)
 
     y_ap = T.pm[:, 0:QP]
-    seq = [i for b in turn for i in range(blocks[b][0], blocks[b][1])]
     last = None
-    for c, i in enumerate(seq):
+    for s, i in enumerate(seq):
         j = order[i]
-        for b in turn:
-            if blocks[b][0] == i:
-                te.wait_ge(sem["tr%d" % b], 1)
+        if s == 0:
+            te.wait_ge(sem.pa0, 1)
+        if s == NA // 2:
+            te.wait_ge(sem.pa1, 1)
+        if s == NA:
+            te.wait_ge(sem.pb, 1)
         if j == rank:
             te.wait_ge(sem.ldv, 16)
         else:
-            te.wait_ge(sem["va%d" % j], eng)
-        last = te.matmul(y_ap, vslot(j), T.p[:, i * QP:(i + 1) * QP], c == 0, c == n - 1)
+            te.wait_ge(sem["va%d" % j], v_count(j)[0])
+        last = te.matmul(y_ap, vslot(j), T.p[:, s * QP:(s + 1) * QP], s == 0, s == n - 1)
     last.then_inc(sem.yd, 1)
     ve.wait_ge(sem.yd, 1)
     ve.tensor_copy(T.ysb[:], y_ap).then_inc(sem.yc, 1)
     g.sync.wait_ge(sem.yc, 1)
     g.sync.dma_start(T.y[:], T.ysb[:]).then_inc(sem.stored, 16)
     g.sync.wait_ge(sem.stored, 16)
-    g.wait_ge(sem.sent, 2 * eng)
+    g.wait_ge(sem.sent, sent)

from concourse.bass import DstId, RemoteDMATransfer
from concourse.mybir import dt, AluOpType, AxisListType, ActivationFunctionType

N = 7
QP = 32
KP = 128
GROUPS = [(0, 3), (3, 5), (5, 6), (6, 7)]
NA = 4

SCRATCH = {
    "kall": ("sbuf", [128, N * KP], "bfloat16"),
    "vall": ("sbuf", [128, N * KP], "bfloat16"),
    "qs": ("sbuf", [128, QP], "bfloat16"),
    "zb": ("sbuf", [128, KP], "bfloat16"),
    "stair": ("sbuf", [128, QP + 1], "bfloat16"),
    "eye": ("sbuf", [128, KP], "bfloat16"),
    "mx": ("sbuf", [128, 4], "float32"),
    "bb": ("sbuf", [128, KP], "bfloat16"),
    "ml": ("sbuf", [128, KP], "bfloat16"),
    "p": ("sbuf", [128, N * QP], "bfloat16"),
    "ysb": ("sbuf", [128, QP], "bfloat16"),
    "pm": ("psum", [128, 512], "float32"),
    "sa": ("psum", [128, 512], "float32"),
    "sb": ("psum", [128, 512], "float32"),
}
for _b in range(len(GROUPS)):
    SCRATCH["t%d" % _b] = ("psum", [128, 512], "float32")

SEMAPHORES = (["ldk", "ldv", "ldq", "sent", "vh", "stored", "zs", "fill0", "fill", "idn", "gz", "ga", "gb",
               "bs", "mls", "ba", "bbs", "pa0", "pa1", "pb", "yd", "yc"]
              + ["ka%d" % j for j in range(N)] + ["va%d" % j for j in range(N)]
              + ["st%d" % j for j in range(len(GROUPS))] + ["rd%d" % j for j in range(len(GROUPS))])

_CACHE = {}


def _way(topo, s, d):
    cs, cd, di = topo.chip(s), topo.chip(d), topo.die(s)
    if cs == cd:
        return ()
    if topo.same_plane(cs, cd):
        return (("out", cs, di), ("in", cd, di))
    if topo.mates(cs, cd):
        return (("mate", cs, di),)
    m = [c for c in range(topo.CHIPS) if topo.mates(cs, c)][0]
    return (("mate", cs, di), ("out", m, di), ("in", cd, di))


def _rounds(topo, cores):
    key = tuple(cores)
    if key not in _CACHE:
        n = len(cores)
        way = {(a, b): _way(topo, cores[a], cores[b]) for a in range(n) for b in range(n) if a != b}
        good = [[] for _d in range(n)]
        perm = [0] * n

        def fill(r, taken, busy):
            if r == n:
                bits = 0
                for a in range(n):
                    bits |= 1 << (a * n + perm[a])
                good[perm[0]].append((bits, tuple(perm)))
                return
            for d in range(n):
                if d == r or d in taken or any(l in busy for l in way[(r, d)]):
                    continue
                perm[r] = d
                fill(r + 1, taken | {d}, busy | set(way[(r, d)]))

        def cover(d0, bits, chosen):
            if d0 == n:
                return chosen
            for b, p in good[d0]:
                if b & bits:
                    continue
                res = cover(d0 + 1, bits | b, chosen + [p])
                if res is not None:
                    return res
            return None

        fill(0, frozenset(), frozenset())
        found = cover(1, 0, [])
        if found is None:
            found = [tuple((r + s) % n for r in range(n)) for s in range(1, n)]
        _CACHE[key] = found
    return _CACHE[key]


def _plan(topo, cores, rounds, r):
    core = cores[r]
    dests = [rd[r] for rd in rounds]
    cand = [c for c in range(topo.CHIPS * topo.CORES_PER_CHIP)
            if topo.chip(c) == topo.chip(core) and c not in cores and topo.die(c) != topo.die(core)
            and all(topo.may_write(c, cores[d]) for d in dests)]
    if len(cand) < 2 or len(dests) != 6:
        return dests, []
    return dests[0:2], [(cand[0], dests[2:4]), (cand[1], dests[4:6])]


def _mask(topo, src, dsts):
    m = topo.mask(src, dsts[0])
    for d in dsts:
        m &= topo.mask(src, d)
    return m


def _bits(m):
    return bin(m).count("1")


def _ids(topo, dsts):
    out = []
    for d in dsts:
        rid, pid, _se = topo.addr(d)
        out.append(DstId(rid=rid, pnc=pid))
    return out


def _chip_mask(topo, cores, rounds, r):
    core = cores[r]
    _direct, helpers = _plan(topo, cores, rounds, r)
    on = _mask(topo, core, [h for h, _ds in helpers])
    off = _mask(topo, core, [cores[rd[r]] for rd in rounds])
    free = on & ~off
    return free if _bits(free) in (1, 2, 4, 8, 16) else on


def rank_program(g, core, T, topo):
    cores = list(T.cores)
    n = len(cores)
    sem = T.sem
    rounds = _rounds(topo, cores)
    rank = T.rank_of(core)

    def kslot(j):
        return T.kall[:, j * KP:(j + 1) * KP]

    def vslot(j):
        return T.vall[:, j * KP:(j + 1) * KP]

    if rank is None:
        for r in range(n):
            _direct, helpers = _plan(topo, cores, rounds, r)
            for h, ds in helpers:
                if h != core:
                    continue
                hm = _mask(topo, core, [cores[d] for d in ds])
                g.wait_ge(sem.vh, _bits(_chip_mask(topo, cores, rounds, r)))
                g.remote_dma_fused(
                    [RemoteDMATransfer(dst_ids=_ids(topo, [cores[d] for d in ds]), dma_engine_mask=hm,
                                       remote_sem=sem["va%d" % r], srcs=[vslot(r)], dsts=[vslot(r) for _d in ds])],
                    local_sem=sem.sent)
                g.wait_ge(sem.sent, _bits(hm))
        return

    te, ve = g.tensor, g.vector

    g.sync.dma_start(kslot(rank), T.k[:]).then_inc(sem.ldk, 16)
    g.scalar.dma_start(vslot(rank), T.v[:]).then_inc(sem.ldv, 16)
    g.sync.dma_start(T.qs[:], T.q[:]).then_inc(sem.ldq, 16)

    dests = [rd[rank] for rd in rounds]
    mask = _mask(topo, core, [cores[d] for d in dests])
    eng = _bits(mask)
    direct, helpers = _plan(topo, cores, rounds, rank)
    sent = 0
    g.wait_ge(sem.ldk, 16)
    g.remote_dma_fused(
        [RemoteDMATransfer(dst_ids=_ids(topo, [cores[d] for d in dests]), dma_engine_mask=mask,
                           remote_sem=sem["ka%d" % rank], srcs=[kslot(rank)], dsts=[kslot(rank) for _d in dests])],
        local_sem=sem.sent)
    sent += eng
    g.wait_ge(sem.ldv, 16)
    if helpers:
        cm = _chip_mask(topo, cores, rounds, rank)
        g.remote_dma_fused(
            [RemoteDMATransfer(dst_ids=_ids(topo, [h for h, _ds in helpers]), dma_engine_mask=cm,
                               remote_sem=sem.vh, srcs=[vslot(rank)], dsts=[vslot(rank) for _h in helpers])],
            local_sem=sem.sent)
        sent += _bits(cm)
    g.remote_dma_fused(
        [RemoteDMATransfer(dst_ids=_ids(topo, [cores[d] for d in direct]), dma_engine_mask=mask,
                           remote_sem=sem["va%d" % rank], srcs=[vslot(rank)], dsts=[vslot(rank) for _d in direct])],
        local_sem=sem.sent)
    sent += eng

    def v_count(j):
        dj, hj = _plan(topo, cores, rounds, j)
        for h, ds in hj:
            if rank in ds:
                return _bits(_mask(topo, h, [cores[d] for d in ds])), False
        return _bits(_mask(topo, cores[j], [cores[rd[j]] for rd in rounds])), True

    ve.memset(T.zb[0:QP, :], 0.0).then_inc(sem.zs, 1)
    ve.memset(T.stair[0:QP, :], 0.0).then_inc(sem.fill0, 1)
    ve.wait_ge(sem.fill0, 1)
    for c in range(QP):
        ve.memset(T.stair[0:c + 1, c + 1:c + 2], -0.5).then_inc(sem.fill, 1)
    ve.wait_ge(sem.fill, QP)
    for a in range(KP // QP):
        ve.tensor_tensor(T.eye[0:QP, a * QP:(a + 1) * QP], T.stair[0:QP, 1:QP + 1], T.stair[0:QP, 0:QP],
                         AluOpType.subtract).then_inc(sem.idn, 1)

    order = [rank] + [list(rd).index(rank) for rd in rounds]
    late = [i for i in range(1, n) if v_count(order[i])[1]]
    seq = [0] + [i for i in range(1, n) if i not in late] + late
    slot = {i: s for s, i in enumerate(seq)}
    wa, wb = NA * QP, (n - NA) * QP

    def s_ap(i):
        s = slot[i]
        return T.sa[:, s * QP:(s + 1) * QP] if s < NA else T.sb[:, (s - NA) * QP:(s - NA + 1) * QP]

    te.wait_ge(sem.zs, 1)
    te.matmul(T.sa[:, 0:wa], T.zb[0:QP, :], T.zb[0:QP, 0:wa], True, False).then_inc(sem.gz, 1)
    te.matmul(T.sb[:, 0:wb], T.zb[0:QP, :], T.zb[0:QP, 0:wb], True, False).then_inc(sem.gz, 1)
    te.wait_ge(sem.gz, 2)

    for b, (lo, hi) in enumerate(GROUPS):
        tb = T["t%d" % b]
        for i in range(lo, hi):
            j = order[i]
            if i == 0:
                te.wait_ge(sem.ldk, 16)
                te.wait_ge(sem.ldq, 16)
            else:
                te.wait_ge(sem["ka%d" % j], eng)
            te.matmul(tb[0:QP, (i - lo) * KP:(i - lo + 1) * KP], T.qs[:], kslot(j), True, True).then_inc(
                sem["st%d" % b], 1)
            te.matmul(s_ap(i), kslot(j), T.qs[:], False, False).then_inc(sem.ga if slot[i] < NA else sem.gb, 1)

    def reduce(b):
        lo, hi = GROUPS[b]
        ve.wait_ge(sem["st%d" % b], hi - lo)
        ve.tensor_reduce(T.mx[0:QP, b:b + 1], T["t%d" % b][0:QP, 0:(hi - lo) * KP], AxisListType.X,
                         AluOpType.max).then_inc(sem["rd%d" % b], 1)

    reduce(0)
    reduce(1)
    reduce(2)
    ve.wait_ge(sem.zs, 1)
    ve.wait_ge(sem.rd0, 1)
    ve.wait_ge(sem.rd1, 1)
    ve.tensor_scalar(T.bb[0:QP, :], T.zb[0:QP, :], T.mx[0:QP, 0:1], T.mx[0:QP, 1:2],
                     AluOpType.add, AluOpType.max).then_inc(sem.bs, 1)
    reduce(3)
    ve.wait_ge(sem.bs, 1)
    ve.wait_ge(sem.rd2, 1)
    ve.wait_ge(sem.rd3, 1)
    ve.tensor_scalar(T.ml[0:QP, :], T.bb[0:QP, :], T.mx[0:QP, 2:3], T.mx[0:QP, 3:4],
                     AluOpType.max, AluOpType.max).then_inc(sem.mls, 1)

    te.wait_ge(sem.idn, KP // QP)
    te.wait_ge(sem.ga, NA)
    te.wait_ge(sem.gb, n - NA)
    te.wait_ge(sem.mls, 1)
    te.matmul(T.sa[:, 0:wa], T.ml[0:QP, :], T.eye[0:QP, 0:wa], False, True).then_inc(sem.ba, 1)
    te.matmul(T.sb[:, 0:wb], T.ml[0:QP, :], T.eye[0:QP, 0:wb], False, True).then_inc(sem.bbs, 1)

    ve.wait_ge(sem.ba, 1)
    ha = wa // 2
    ve.tensor_scalar(T.p[:, 0:ha], T.sa[:, 0:ha], 0.0, None, AluOpType.max).then_inc(sem.pa0, 1)
    ve.tensor_scalar(T.p[:, ha:wa], T.sa[:, ha:wa], 0.0, None, AluOpType.max).then_inc(sem.pa1, 1)
    g.scalar.wait_ge(sem.bbs, 1)
    g.scalar.activation(T.p[:, wa:wa + wb], T.sb[:, 0:wb], ActivationFunctionType.Relu).then_inc(sem.pb, 1)

    y_ap = T.pm[:, 0:QP]
    last = None
    for s, i in enumerate(seq):
        j = order[i]
        if s == 0:
            te.wait_ge(sem.pa0, 1)
        if s == NA // 2:
            te.wait_ge(sem.pa1, 1)
        if s == NA:
            te.wait_ge(sem.pb, 1)
        if j == rank:
            te.wait_ge(sem.ldv, 16)
        else:
            te.wait_ge(sem["va%d" % j], v_count(j)[0])
        last = te.matmul(y_ap, vslot(j), T.p[:, s * QP:(s + 1) * QP], s == 0, s == n - 1)
    last.then_inc(sem.yd, 1)
    ve.wait_ge(sem.yd, 1)
    ve.tensor_copy(T.ysb[:], y_ap).then_inc(sem.yc, 1)
    g.sync.wait_ge(sem.yc, 1)
    g.sync.dma_start(T.y[:], T.ysb[:]).then_inc(sem.stored, 16)
    g.sync.wait_ge(sem.stored, 16)
    g.wait_ge(sem.sent, sent)
